import numpy as np
import ml_dtypes


def mxq(x, axis, fmt="e4m3"):
    dtype, down = {"e4m3": (ml_dtypes.float8_e4m3fn, 7), "e5m2": (ml_dtypes.float8_e5m2, 14)}[fmt]
    v = np.moveaxis(np.asarray(x, np.float32).astype(ml_dtypes.bfloat16).astype(np.float64), axis, -1)
    blocks = v.reshape(v.shape[:-1] + (-1, 32))
    amax = np.abs(blocks).max(-1, keepdims=True)
    byte = np.maximum(np.where(amax > 0, np.frexp(amax)[1] - 1 + 127, 0) - down, 1)
    scale = np.exp2(byte - 127.0)
    codes = (blocks / scale).astype(np.float32).astype(dtype).astype(np.float64)
    return np.moveaxis((codes * scale).reshape(v.shape), -1, axis)


WIDE = False


def mx_kscale(k, group=512):
    if not WIDE:
        return np.ones(k)
    levels = np.array([18, -18])
    if group != 512:
        return np.exp2(np.random.permutation(np.resize(levels, k // group))).repeat(group)
    if k % 512:
        return np.exp2(np.random.permutation(np.resize(levels, k // 32))).repeat(32)
    a = np.empty((k // 512, 16))
    for p in range(k // 512):
        a[p, :8] = np.random.permutation(np.resize(levels, 8))
        for g in range(8):
            far = levels[np.abs(levels - a[p, g]) >= 10]
            a[p, g + 8] = far[np.random.randint(len(far))]
    return np.exp2(a.ravel()).repeat(32)


def f64(x):
    return np.asarray(x).astype(np.float64)


def sigmoid(v):
    return 1.0 / (1.0 + np.exp(-v))


G, D, I, Q, E = 8, 128, 128, 128, 128


def sgn(shape):
    return np.random.uniform(0.5, 2.0, shape) * np.where(np.random.standard_normal(shape) < 0, -1.0, 1.0)


def setup_inputs():
    n = np.random.standard_normal
    s_d = mx_kscale(D, 0)
    s_i = mx_kscale(I, 0)
    return {
        "kT": (n((G, D, I)) / np.sqrt(D) / s_d[:, None]).astype(np.float32),
        "qT": (n((G, D, Q)) * s_d[:, None]).astype(np.float32),
        "kb": (n((G, I, 1))).astype(np.float32),
        "t": (sgn((G, I, 1)) * s_i[:, None]).astype(np.float32),
        "v": ((n((G, I, E))) / s_i[:, None]).astype(np.float32),
        "og": (n((G, Q, E))).astype(np.float32),
    }


def reference(kT, qT, kb, t, v, og):
    kTq = mxq(f64(kT), 1, "e4m3")
    qTq = mxq(f64(qT), 1, "e4m3")
    z = kTq.transpose(0, 2, 1) @ qTq
    p = sigmoid(z + f64(kb)) * f64(t)
    pq = mxq(p, 1, "e4m3")
    vq = mxq(f64(v), 1, "e4m3")
    y = pq.transpose(0, 2, 1) @ vq
    o = y / 16.0 * sigmoid(f64(og))
    return o

@@ -1,0 +1,128 @@
+from contextlib import ExitStack
+
+import concourse.mybir as mybir
+
+F32 = mybir.dt.float32
+BF16 = mybir.dt.bfloat16
+U32 = mybir.dt.uint32
+U8 = mybir.dt.uint8
+FP8X4 = mybir.dt.float8_e4m3fn_x4
+SIGMOID = mybir.ActivationFunctionType.Sigmoid
+MULT = mybir.AluOpType.mult
+
+G, W = 8, 128
+P = 128
+PACK = 4
+ROWS = W // PACK
+SIDE = P // ROWS
+SETS = G // SIDE
+LINE = 4
+
+FLOPS = 2 * 2 * G * W * W * W
+
+
+def tile_rows_win_sig_gate_kernel(tc, kT, qT, kb, t, v, og, out):
+    nc = tc.nc
+
+    with ExitStack() as ctx:
+        sb = ctx.enter_context(tc.tile_pool(name="sb", bufs=1))
+        ps = ctx.enter_context(tc.psum_pool(name="ps", bufs=1))
+        ctx.enter_context(tc.manual_schedule())
+
+        def tiles(name, count, shape, dtype):
+            return [sb.tile(shape, dtype, name="%s%d" % (name, n), align_bytes=64) for n in range(count)]
+
+        k_raw = tiles("k_raw", SETS, [P, PACK * W], F32)
+        q_raw = tiles("q_raw", SETS, [P, PACK * W], F32)
+        v_raw = tiles("v_raw", SETS, [P, PACK * W], F32)
+        og_raw = tiles("og_raw", SETS, [P, SIDE * W], F32)
+        gate = tiles("gate", SETS, [P, SIDE * W], F32)
+        result = tiles("result", G, [P, W], F32)
+        sig = tiles("sig", G, [P, W], F32)
+        p_tok = tiles("p_tok", G, [P, W], BF16)
+        p_rows = tiles("p_rows", SETS, [P, PACK * W], BF16)
+        packed = {n: tiles(n + "_bf", SETS, [P, PACK * W], BF16) for n in "kqvp"}
+        codes = {n: tiles(n + "_codes", SETS, [P, W], U32) for n in "kqvp"}
+        scales = {n: tiles(n + "_scales", SETS, [P, W], U8) for n in "kqvp"}
+        kb_t_rows = sb.tile([P, ROWS], F32, align_bytes=64)
+        kb_t = sb.tile([P, ROWS], F32, align_bytes=64)
+        bank = [ps.tile([P, 512], F32, name="bank%d" % g) for g in range(G)]
+
+        def load_rows(dst, src, s):
+            nc.sync.dma_start(out=dst[s][:], in_=src[SIDE * s : SIDE * (s + 1)].rearrange("g (p j) c -> (g p) (j c)", j=PACK))
+
+        def interleave(engine_copy, name, src, s):
+            engine_copy(
+                out=packed[name][s][:].rearrange("p (c i j) -> p c j i", i=LINE, j=PACK),
+                in_=src[s][:].rearrange("p (j c i) -> p c j i", i=LINE, j=PACK),
+            )
+
+        def quantize(name, s):
+            nc.vector.quantize_mx(out=codes[name][s][:].bitcast(FP8X4), scales=scales[name][s][:], in_=packed[name][s][:])
+
+        def product(dst, stationary, moving, g):
+            s, r = divmod(g, SIDE)
+            rows = slice(ROWS * r, ROWS * (r + 1))
+            nc.tensor.matmul_mx(
+                out=dst,
+                lhsT=codes[stationary][s][rows, :].bitcast(FP8X4),
+                lhsT_scale=scales[stationary][s][rows, :],
+                rhs=codes[moving][s][rows, :].bitcast(FP8X4),
+                rhs_scale=scales[moving][s][rows, :],
+                start=True,
+                stop=True,
+            )
+
+        def windows(s):
+            return range(SIDE * s, SIDE * (s + 1))
+
+        nc.vector.memset(kb_t_rows[:], 0.0)
+        nc.scalar.dma_start(out=kb_t_rows[0:P:4, :], in_=kb.rearrange("g (a c) o -> a g (c o)", c=ROWS))
+        nc.scalar.dma_start(out=kb_t_rows[1:P:4, :], in_=t.rearrange("g (a c) o -> a g (c o)", c=ROWS))
+        for s in range(SETS):
+            load_rows(k_raw, kT, s)
+            load_rows(q_raw, qT, s)
+        for s in range(SETS):
+            load_rows(v_raw, v, s)
+        for s in range(SETS):
+            nc.sync.dma_start(
+                out=og_raw[s][:].rearrange("q (g e) -> q g e", g=SIDE),
+                in_=og[SIDE * s : SIDE * (s + 1)].rearrange("g q e -> q g e"),
+            )
+
+        nc.vector.transpose(out=kb_t[:], in_=kb_t_rows[:])
+
+        for s in range(SETS):
+            interleave(nc.vector.tensor_copy, "k", k_raw, s)
+            interleave(nc.vector.tensor_copy, "q", q_raw, s)
+            quantize("k", s)
+            quantize("q", s)
+            for g in windows(s):
+                product(bank[g][:, 0:W], "k", "q", g)
+
+        for g in range(G):
+            s, r = divmod(g, SIDE)
+            nc.scalar.activation(out=sig[g][:], in_=bank[g][:, 0:W], func=SIGMOID, bias=kb_t[:, 4 * g : 4 * g + 1])
+            nc.vector.tensor_scalar(out=p_tok[g][:], in0=sig[g][:], scalar1=kb_t[:, 4 * g + 1 : 4 * g + 2], scalar2=None, op0=MULT)
+            nc.sync.dma_start(
+                out=p_rows[s][ROWS * r : ROWS * (r + 1), :].rearrange("p (j c) -> p j c", j=PACK),
+                in_=p_tok[g][:],
+            )
+
+        for s in range(SETS):
+            interleave(nc.scalar.copy, "v", v_raw, s)
+            nc.scalar.activation(out=gate[s][:], in_=og_raw[s][:], func=SIGMOID)
+
+        for s in range(SETS):
+            interleave(nc.vector.tensor_copy, "p", p_rows, s)
+            quantize("v", s)
+            quantize("p", s)
+            for g in windows(s):
+                product(bank[g][:, W : 2 * W], "p", "v", g)
+
+        for g in range(G):
+            s, r = divmod(g, SIDE)
+            nc.vector.scalar_tensor_tensor(
+                out=result[g][:], in0=bank[g][:, W : 2 * W], scalar=1.0 / 16.0, in1=gate[s][:, W * r : W * (r + 1)], op0=MULT, op1=MULT
+            )
+            nc.sync.dma_start(out=out[g], in_=result[g][:])

@@ -34,8 +34,9 @@ def tile_rows_win_sig_gate_kernel(tc, kT, qT, kb, t, v, og, out):
 
         k_raw = tiles("k_raw", SETS, [P, PACK * W], F32)
         q_raw = tiles("q_raw", SETS, [P, PACK * W], F32)
-        v_raw = tiles("v_raw", SETS, [P, PACK * W], F32)
-        og_raw = tiles("og_raw", SETS, [P, SIDE * W], F32)
+        v_all = sb.tile([P, SETS, PACK * W], F32, align_bytes=64)
+        og_all = sb.tile([P, G * W], F32, align_bytes=64)
+        v_raw = [v_all[:, s, :] for s in range(SETS)]
         gate = tiles("gate", SETS, [P, SIDE * W], F32)
         result = tiles("result", G, [P, W], F32)
         sig = tiles("sig", G, [P, W], F32)
@@ -49,12 +50,12 @@ def tile_rows_win_sig_gate_kernel(tc, kT, qT, kb, t, v, og, out):
         bank = [ps.tile([P, 512], F32, name="bank%d" % g) for g in range(G)]
 
         def load_rows(dst, src, s):
-            nc.sync.dma_start(out=dst[s][:], in_=src[SIDE * s : SIDE * (s + 1)].rearrange("g (p j) c -> (g p) (j c)", j=PACK))
+            nc.scalar.dma_start(out=dst[s][:], in_=src[SIDE * s : SIDE * (s + 1)].rearrange("g (p j) c -> (g p) (j c)", j=PACK))
 
         def interleave(engine_copy, name, src, s):
             engine_copy(
                 out=packed[name][s][:].rearrange("p (c i j) -> p c j i", i=LINE, j=PACK),
-                in_=src[s][:].rearrange("p (j c i) -> p c j i", i=LINE, j=PACK),
+                in_=src[s][:, :].rearrange("p (j c i) -> p c j i", i=LINE, j=PACK),
             )
 
         def quantize(name, s):
@@ -76,31 +77,7 @@ def tile_rows_win_sig_gate_kernel(tc, kT, qT, kb, t, v, og, out):
         def windows(s):
             return range(SIDE * s, SIDE * (s + 1))
 
-        nc.vector.memset(kb_t_rows[:], 0.0)
-        nc.scalar.dma_start(out=kb_t_rows[0:P:4, :], in_=kb.rearrange("g (a c) o -> a g (c o)", c=ROWS))
-        nc.scalar.dma_start(out=kb_t_rows[1:P:4, :], in_=t.rearrange("g (a c) o -> a g (c o)", c=ROWS))
-        for s in range(SETS):
-            load_rows(k_raw, kT, s)
-            load_rows(q_raw, qT, s)
-        for s in range(SETS):
-            load_rows(v_raw, v, s)
-        for s in range(SETS):
-            nc.sync.dma_start(
-                out=og_raw[s][:].rearrange("q (g e) -> q g e", g=SIDE),
-                in_=og[SIDE * s : SIDE * (s + 1)].rearrange("g q e -> q g e"),
-            )
-
-        nc.vector.transpose(out=kb_t[:], in_=kb_t_rows[:])
-
-        for s in range(SETS):
-            interleave(nc.vector.tensor_copy, "k", k_raw, s)
-            interleave(nc.vector.tensor_copy, "q", q_raw, s)
-            quantize("k", s)
-            quantize("q", s)
-            for g in windows(s):
-                product(bank[g][:, 0:W], "k", "q", g)
-
-        for g in range(G):
+        def weigh(g):
             s, r = divmod(g, SIDE)
             nc.scalar.activation(out=sig[g][:], in_=bank[g][:, 0:W], func=SIGMOID, bias=kb_t[:, 4 * g : 4 * g + 1])
             nc.vector.tensor_scalar(out=p_tok[g][:], in0=sig[g][:], scalar1=kb_t[:, 4 * g + 1 : 4 * g + 2], scalar2=None, op0=MULT)
@@ -109,20 +86,53 @@ def tile_rows_win_sig_gate_kernel(tc, kT, qT, kb, t, v, og, out):
                 in_=p_tok[g][:],
             )
 
-        for s in range(SETS):
-            interleave(nc.scalar.copy, "v", v_raw, s)
-            nc.scalar.activation(out=gate[s][:], in_=og_raw[s][:], func=SIGMOID)
-
-        for s in range(SETS):
-            interleave(nc.vector.tensor_copy, "p", p_rows, s)
-            quantize("v", s)
-            quantize("p", s)
-            for g in windows(s):
-                product(bank[g][:, W : 2 * W], "p", "v", g)
-
-        for g in range(G):
+        def finish(g):
             s, r = divmod(g, SIDE)
             nc.vector.scalar_tensor_tensor(
                 out=result[g][:], in0=bank[g][:, W : 2 * W], scalar=1.0 / 16.0, in1=gate[s][:, W * r : W * (r + 1)], op0=MULT, op1=MULT
             )
             nc.sync.dma_start(out=out[g], in_=result[g][:])
+
+        nc.vector.memset(kb_t_rows[:], 0.0)
+        for s in range(SETS):
+            load_rows(k_raw, kT, s)
+            load_rows(q_raw, qT, s)
+        nc.scalar.dma_start(out=v_all[:], in_=v.rearrange("(s g) (p j) c -> (g p) s (j c)", s=SETS, j=PACK))
+        nc.scalar.dma_start(out=og_all[:].rearrange("q (g e) -> q g e", g=G), in_=og.rearrange("g q e -> q g e"))
+        warm = sb.tile([P, 2], F32, align_bytes=64)
+        nc.vector.memset(warm[:, 0:1], 0.0)
+        nc.scalar.activation(out=warm[:, 1:2], in_=warm[:, 0:1], func=SIGMOID)
+        nc.sync.dma_start(out=kb_t_rows[0:P:4, :], in_=kb.rearrange("g (a c) o -> a g (c o)", c=ROWS))
+        nc.sync.dma_start(out=kb_t_rows[1:P:4, :], in_=t.rearrange("g (a c) o -> a g (c o)", c=ROWS))
+
+        for s in range(SETS):
+            interleave(nc.vector.tensor_copy, "k", k_raw, s)
+            interleave(nc.vector.tensor_copy, "q", q_raw, s)
+            quantize("k", s)
+            quantize("q", s)
+            if s == 0:
+                nc.vector.transpose(out=kb_t[:], in_=kb_t_rows[:])
+            for g in windows(s):
+                product(bank[g][:, 0:W], "k", "q", g)
+
+        for g in range(G):
+            weigh(g)
+
+        interleave(nc.vector.tensor_copy, "v", v_raw, 0)
+        interleave(nc.scalar.copy, "v", v_raw, 1)
+        for s in range(SETS):
+            nc.scalar.activation(out=gate[s][:], in_=og_all[:, SIDE * W * s : SIDE * W * (s + 1)], func=SIGMOID)
+
+        interleave(nc.vector.tensor_copy, "p", p_rows, 0)
+        quantize("v", 0)
+        quantize("p", 0)
+        for g in windows(0):
+            product(bank[g][:, W : 2 * W], "p", "v", g)
+        quantize("v", 1)
+        interleave(nc.vector.tensor_copy, "p", p_rows, 1)
+        finish(0)
+        quantize("p", 1)
+        for g in windows(1):
+            product(bank[g][:, W : 2 * W], "p", "v", g)
+        for g in range(1, G):
+            finish(g)

from contextlib import ExitStack

import concourse.mybir as mybir

F32 = mybir.dt.float32
BF16 = mybir.dt.bfloat16
U32 = mybir.dt.uint32
U8 = mybir.dt.uint8
FP8X4 = mybir.dt.float8_e4m3fn_x4
SIGMOID = mybir.ActivationFunctionType.Sigmoid
MULT = mybir.AluOpType.mult

G, W = 8, 128
P = 128
PACK = 4
ROWS = W // PACK
SIDE = P // ROWS
SETS = G // SIDE
LINE = 4

FLOPS = 2 * 2 * G * W * W * W


def tile_rows_win_sig_gate_kernel(tc, kT, qT, kb, t, v, og, out):
    nc = tc.nc

    with ExitStack() as ctx:
        sb = ctx.enter_context(tc.tile_pool(name="sb", bufs=1))
        ps = ctx.enter_context(tc.psum_pool(name="ps", bufs=1))
        ctx.enter_context(tc.manual_schedule())

        def tiles(name, count, shape, dtype):
            return [sb.tile(shape, dtype, name="%s%d" % (name, n), align_bytes=64) for n in range(count)]

        k_raw = tiles("k_raw", SETS, [P, PACK * W], F32)
        q_raw = tiles("q_raw", SETS, [P, PACK * W], F32)
        v_all = sb.tile([P, SETS, PACK * W], F32, align_bytes=64)
        og_all = sb.tile([P, G * W], F32, align_bytes=64)
        v_raw = [v_all[:, s, :] for s in range(SETS)]
        gate = tiles("gate", SETS, [P, SIDE * W], F32)
        result = tiles("result", G, [P, W], F32)
        sig = tiles("sig", G, [P, W], F32)
        p_tok = tiles("p_tok", G, [P, W], BF16)
        p_rows = tiles("p_rows", SETS, [P, PACK * W], BF16)
        packed = {n: tiles(n + "_bf", SETS, [P, PACK * W], BF16) for n in "kqvp"}
        codes = {n: tiles(n + "_codes", SETS, [P, W], U32) for n in "kqvp"}
        scales = {n: tiles(n + "_scales", SETS, [P, W], U8) for n in "kqvp"}
        kb_t_rows = sb.tile([P, ROWS], F32, align_bytes=64)
        kb_t = sb.tile([P, ROWS], F32, align_bytes=64)
        bank = [ps.tile([P, 512], F32, name="bank%d" % g) for g in range(G)]

        def load_rows(dst, src, s):
            nc.scalar.dma_start(out=dst[s][:], in_=src[SIDE * s : SIDE * (s + 1)].rearrange("g (p j) c -> (g p) (j c)", j=PACK))

        def interleave(engine_copy, name, src, s):
            engine_copy(
                out=packed[name][s][:].rearrange("p (c i j) -> p c j i", i=LINE, j=PACK),
                in_=src[s][:, :].rearrange("p (j c i) -> p c j i", i=LINE, j=PACK),
            )

        def quantize(name, s):
            nc.vector.quantize_mx(out=codes[name][s][:].bitcast(FP8X4), scales=scales[name][s][:], in_=packed[name][s][:])

        def product(dst, stationary, moving, g):
            s, r = divmod(g, SIDE)
            rows = slice(ROWS * r, ROWS * (r + 1))
            nc.tensor.matmul_mx(
                out=dst,
                lhsT=codes[stationary][s][rows, :].bitcast(FP8X4),
                lhsT_scale=scales[stationary][s][rows, :],
                rhs=codes[moving][s][rows, :].bitcast(FP8X4),
                rhs_scale=scales[moving][s][rows, :],
                start=True,
                stop=True,
            )

        def windows(s):
            return range(SIDE * s, SIDE * (s + 1))

        def weigh(g):
            s, r = divmod(g, SIDE)
            nc.scalar.activation(out=sig[g][:], in_=bank[g][:, 0:W], func=SIGMOID, bias=kb_t[:, 4 * g : 4 * g + 1])
            nc.vector.tensor_scalar(out=p_tok[g][:], in0=sig[g][:], scalar1=kb_t[:, 4 * g + 1 : 4 * g + 2], scalar2=None, op0=MULT)
            nc.sync.dma_start(
                out=p_rows[s][ROWS * r : ROWS * (r + 1), :].rearrange("p (j c) -> p j c", j=PACK),
                in_=p_tok[g][:],
            )

        def finish(g):
            s, r = divmod(g, SIDE)
            nc.vector.scalar_tensor_tensor(
                out=result[g][:], in0=bank[g][:, W : 2 * W], scalar=1.0 / 16.0, in1=gate[s][:, W * r : W * (r + 1)], op0=MULT, op1=MULT
            )
            nc.sync.dma_start(out=out[g], in_=result[g][:])

        nc.vector.memset(kb_t_rows[:], 0.0)
        for s in range(SETS):
            load_rows(k_raw, kT, s)
            load_rows(q_raw, qT, s)
        nc.scalar.dma_start(out=v_all[:], in_=v.rearrange("(s g) (p j) c -> (g p) s (j c)", s=SETS, j=PACK))
        nc.scalar.dma_start(out=og_all[:].rearrange("q (g e) -> q g e", g=G), in_=og.rearrange("g q e -> q g e"))
        warm = sb.tile([P, 2], F32, align_bytes=64)
        nc.vector.memset(warm[:, 0:1], 0.0)
        nc.scalar.activation(out=warm[:, 1:2], in_=warm[:, 0:1], func=SIGMOID)
        nc.sync.dma_start(out=kb_t_rows[0:P:4, :], in_=kb.rearrange("g (a c) o -> a g (c o)", c=ROWS))
        nc.sync.dma_start(out=kb_t_rows[1:P:4, :], in_=t.rearrange("g (a c) o -> a g (c o)", c=ROWS))

        for s in range(SETS):
            interleave(nc.vector.tensor_copy, "k", k_raw, s)
            interleave(nc.vector.tensor_copy, "q", q_raw, s)
            quantize("k", s)
            quantize("q", s)
            if s == 0:
                nc.vector.transpose(out=kb_t[:], in_=kb_t_rows[:])
            for g in windows(s):
                product(bank[g][:, 0:W], "k", "q", g)

        for g in range(G):
            weigh(g)

        interleave(nc.vector.tensor_copy, "v", v_raw, 0)
        interleave(nc.scalar.copy, "v", v_raw, 1)
        for s in range(SETS):
            nc.scalar.activation(out=gate[s][:], in_=og_all[:, SIDE * W * s : SIDE * W * (s + 1)], func=SIGMOID)

        interleave(nc.vector.tensor_copy, "p", p_rows, 0)
        quantize("v", 0)
        quantize("p", 0)
        for g in windows(0):
            product(bank[g][:, W : 2 * W], "p", "v", g)
        quantize("v", 1)
        interleave(nc.vector.tensor_copy, "p", p_rows, 1)
        finish(0)
        quantize("p", 1)
        for g in windows(1):
            product(bank[g][:, W : 2 * W], "p", "v", g)
        for g in range(1, G):
            finish(g)
